import numpy as np
import ml_dtypes


def mxq(x, axis, fmt="e4m3"):
    dtype, down = {"e4m3": (ml_dtypes.float8_e4m3fn, 7), "e5m2": (ml_dtypes.float8_e5m2, 14)}[fmt]
    v = np.moveaxis(np.asarray(x, np.float32).astype(ml_dtypes.bfloat16).astype(np.float64), axis, -1)
    blocks = v.reshape(v.shape[:-1] + (-1, 32))
    amax = np.abs(blocks).max(-1, keepdims=True)
    byte = np.maximum(np.where(amax > 0, np.frexp(amax)[1] - 1 + 127, 0) - down, 1)
    scale = np.exp2(byte - 127.0)
    codes = (blocks / scale).astype(np.float32).astype(dtype).astype(np.float64)
    return np.moveaxis((codes * scale).reshape(v.shape), -1, axis)


WIDE = False


def mx_kscale(k):
    if not WIDE:
        return np.ones(k)
    levels = np.array([10, -10, 5, -5, 0])
    if k % 512:
        return np.exp2(np.random.permutation(np.resize(levels, k // 32))).repeat(32)
    a = np.empty((k // 512, 16))
    for p in range(k // 512):
        a[p, :8] = np.random.permutation(np.resize(levels, 8))
        for g in range(8):
            far = levels[np.abs(levels - a[p, g]) >= 10]
            a[p, g + 8] = far[np.random.randint(len(far))]
    return np.exp2(a.ravel()).repeat(32)


def f64(x):
    return np.asarray(x).astype(np.float64)


def striped(idx):
    return np.tile(idx.reshape(-1, 16).T, (8, 1)).astype(np.uint16)


def unstriped(offs):
    return offs[:16].T.reshape(-1).astype(np.int64)


def pack_weight(w):
    k, n = w.shape
    w = f64(np.asarray(w, np.float32).astype(ml_dtypes.bfloat16)).reshape(k // 32, 32, n)
    amax = np.abs(w).max(1)
    byte = np.clip(np.where(amax > 0, np.frexp(amax)[1] - 1 + 127 - 7, 1), 1, 254)
    scaled = (w * np.exp2(127.0 - byte)[:, None, :]).reshape(k, n).astype(np.float32)
    words = np.ascontiguousarray(scaled.reshape(k // 512, 128, 4, n).transpose(0, 1, 3, 2)).astype(ml_dtypes.float8_e4m3fn).view(np.uint8)
    return words, np.ascontiguousarray(byte.astype(np.uint8).reshape(k // 512, 16, n))


def unpack_weight(words, scales):
    g, p, n, _ = words.shape
    vals = np.ascontiguousarray(words).view(ml_dtypes.float8_e4m3fn).astype(np.float64) * np.repeat(np.exp2(scales.astype(np.float64) - 127.0), 8, axis=1)[..., None]
    return vals.transpose(0, 1, 3, 2).reshape(g * 512, n)


def sigmoid(v):
    return 1.0 / (1.0 + np.exp(-np.maximum(v, -700.0)))


K, T, S, D, H, Z, W = 512, 2048, 512, 2, 512, 512, 2048
P = 2 ** 7


def setup_inputs():
    n = np.random.standard_normal
    s = mx_kscale(K)[:, None]
    packed_xT = pack_weight(n((K, T)) * s)
    packed_eT = pack_weight(n((K, W)) * s)
    return {
        "x_words": packed_xT[0],
        "x_scales": packed_xT[1],
        "w1": (n((K, H)) / np.sqrt(K) / s).astype(np.float32),
        "w2": (n((K, H)) / np.sqrt(K) / s).astype(np.float32),
        "e_words": packed_eT[0],
        "e_scales": packed_eT[1],
        "unit": (np.random.uniform(0.6, 1.4, (K, 1)) / np.sqrt(K) / s).astype(np.float32),
        "price": (np.tile(np.random.uniform(0.2, 1.4, W), (P, 1))).astype(np.float32),
        "offs": striped(np.random.permutation(T)[:S]),
        "sub_": striped(np.random.permutation(S)),
        "off": striped(np.random.permutation(W)[:Z]),
        "cmp": striped(np.random.permutation(Z)),
    }


def reference(x_words, x_scales, w1, w2, e_words, e_scales, unit, price, offs, sub_, off, cmp):
    xq = unpack_weight(x_words, x_scales)[:, unstriped(offs)]
    y = mxq(f64(w1), 0, "e4m3").T @ xq
    yg = mxq(f64(w2), 0, "e4m3").T @ xq
    gs = yg[:, unstriped(sub_)]
    aug = y + 0.6 * gs
    bask = aug.reshape(len(aug), -1, D).sum(axis=2)
    bq = np.tanh(bask) * (np.abs(bask) + 0.4)
    hid = f64(unit) * bq
    e_off = unpack_weight(e_words, e_scales)[:, unstriped(off)]
    sc = mxq(hid, 0, "e4m3").T @ e_off
    syn = sc + 0.5 * sc[:, unstriped(cmp)]
    surp = syn - (f64(price)[:1][:, unstriped(off)])
    return sigmoid(surp) * (f64(price)[:1][:, unstriped(off)])

@@ -1,0 +1,240 @@
+from contextlib import ExitStack
+
+import concourse.mybir as mybir
+
+F32 = mybir.dt.float32
+BF16 = mybir.dt.bfloat16
+I32 = mybir.dt.int32
+U32 = mybir.dt.uint32
+U16 = mybir.dt.uint16
+U8 = mybir.dt.uint8
+FP8X4 = mybir.dt.float8_e4m3fn_x4
+ALU = mybir.AluOpType
+ACT = mybir.ActivationFunctionType
+
+P = 128
+PACK = 4
+K = 512
+TABLE = 2048
+PICKED = 512
+HALF = 256
+LIST_COLS = PICKED // 16
+FLOPS = 2 * K * 512 * PICKED * 2 + 2 * 512 * 256 * PICKED
+
+
+def tile_picked_ybundle_rev_p_kernel(
+    tc, x_words, x_scales, w1, w2, e_words, e_scales, unit, price, offs, sub_, off, cmp, out
+):
+    nc = tc.nc
+    with ExitStack() as ctx:
+        lists = ctx.enter_context(tc.tile_pool(name="lists", bufs=1))
+        sb = ctx.enter_context(tc.tile_pool(name="sb", bufs=1))
+        reuse = ctx.enter_context(tc.tile_pool(name="reuse", bufs=1))
+        psum = ctx.enter_context(tc.psum_pool(name="psum", bufs=1))
+
+        def load_list(src, name):
+            t = lists.tile([P, LIST_COLS], U16, name=name)
+            nc.sync.dma_start(t[:], src)
+            return t
+
+        def half_list(lst, h):
+            return lst[:, h * (LIST_COLS // 2) : (h + 1) * (LIST_COLS // 2)]
+
+        def half(h):
+            return slice(h * HALF, (h + 1) * HALF)
+
+        def load_scale_table(t, src, clear_engine):
+            as_words = t[:].bitcast(I32)
+            clear_engine.memset(as_words, 0)
+            rows = src[0].bitcast(I32)
+            for q in range(4):
+                nc.sync.dma_start(as_words[32 * q : 32 * q + 4, :], rows[4 * q : 4 * q + 4, :])
+
+        def load_word_table(t, src):
+            nc.sync.dma_start(t[:].bitcast(I32), src[0].rearrange("p n t -> p (n t)").bitcast(I32))
+
+        def load_weight(t, src):
+            nc.sync.dma_start(t[:], src.rearrange("(p j) c -> p j c", j=PACK))
+
+        def round_weight(raw, grouped, engine_copy, m0, m1):
+            engine_copy(
+                grouped[:].rearrange("p t m j -> p m j t")[:, m0:m1],
+                raw[:].rearrange("p j (m t) -> p m j t", t=PACK)[:, m0:m1],
+            )
+
+        def quantize(grouped_ap, width, name, tag=""):
+            codes = sb.tile([P, width], U32, name=name + "_codes", tag=tag, align_bytes=64)
+            scales = sb.tile([P, width], U8, name=name + "_scales", align_bytes=64)
+            nc.vector.quantize_mx(out=codes[:].bitcast(FP8X4), scales=scales[:], in_=grouped_ap)
+            return codes, scales
+
+        def mm(acc, lhs, lcols, rhs, rcols, start, stop):
+            nc.tensor.matmul_mx(
+                out=acc,
+                lhsT=lhs[0][:, lcols].bitcast(FP8X4),
+                lhsT_scale=lhs[1][:, lcols],
+                rhs=rhs[0][:, rcols].bitcast(FP8X4),
+                rhs_scale=rhs[1][:, rcols],
+                start=start,
+                stop=stop,
+            )
+
+        unit_t = reuse.tile([P, PACK], F32, name="unit_t", offset=0, align_bytes=64)
+        nc.sync.dma_start(unit_t[:], unit.rearrange("(p t) o -> p (t o)", t=PACK))
+        offs_t = load_list(offs, "offs_t")
+        off_t = load_list(off, "off_t")
+        w2_raw = sb.tile([P, PACK, 512], F32, name="w2_raw", tag="buf_c", align_bytes=64)
+        load_weight(w2_raw, w2)
+        sub_t = load_list(sub_, "sub_t")
+        cmp_t = load_list(cmp, "cmp_t")
+        xs_table = sb.tile([P, TABLE], U8, name="xs_table", tag="buf_d", align_bytes=64)
+        load_scale_table(xs_table, x_scales, nc.vector)
+
+        positive = sb.tile([P, PACK], F32, name="positive", tag="buf_b")
+        nc.vector.tensor_scalar(positive[:], unit_t[:], 0.0, 2.0, ALU.is_ge, ALU.mult)
+        unit_abs = sb.tile([P, PACK], F32, name="unit_abs")
+        nc.scalar.activation(unit_abs[:], unit_t[:], ACT.Abs)
+        unit_off = sb.tile([P, PACK], F32, name="unit_off")
+        nc.scalar.activation(unit_off[:], unit_t[:], ACT.Abs, scale=0.4)
+        unit_sign = sb.tile([P, PACK], F32, name="unit_sign")
+        nc.scalar.activation(unit_sign[:], positive[:], ACT.Copy, bias=-1.0)
+
+        xw_table = reuse.tile([P, TABLE], U32, name="xw_table", offset=0, align_bytes=64)
+        load_word_table(xw_table, x_words)
+        w1_raw = sb.tile([P, PACK, 512], F32, name="w1_raw", tag="buf_b")
+        load_weight(w1_raw, w1)
+
+        w2_grouped = sb.tile([P, PACK, P, PACK], BF16, name="w2_grouped", align_bytes=64)
+        round_weight(w2_raw, w2_grouped, nc.vector.tensor_copy, 0, 40)
+        round_weight(w2_raw, w2_grouped, nc.scalar.copy, 40, P)
+        xs = sb.tile([P, PICKED], U8, name="xs", align_bytes=64)
+        nc.vector.tensor_copy(xs[:], xs_table[:].indirect(offs_t[:]))
+        es_table = sb.tile([P, TABLE], U8, name="es_table", tag="buf_c", align_bytes=64)
+        load_scale_table(es_table, e_scales, nc.gpsimd)
+        w2q = quantize(w2_grouped[:].rearrange("p t m j -> p (t m j)"), 512, "w2q", "buf_d")
+
+        xw = []
+        for h in range(2):
+            picked = sb.tile([P, HALF], U32, name="xw%d" % h, align_bytes=64)
+            nc.vector.tensor_copy(picked[:], xw_table[:].indirect(half_list(offs_t, h)))
+            xw.append(picked)
+
+        ew_table = reuse.tile([P, TABLE], U32, name="ew_table", offset=3 * TABLE, align_bytes=64)
+        load_word_table(ew_table, e_words)
+
+        yg_ps = [psum.tile([P, PICKED], F32, name="yg_ps%d" % t, tag="bank%d" % t) for t in range(PACK)]
+        for pair in range(2):
+            for h in range(2):
+                for t in (2 * pair, 2 * pair + 1):
+                    mm(yg_ps[t][:, half(h)], w2q, slice(t * P, (t + 1) * P), (xw[h], xs[:, half(h)]), slice(0, HALF), True, True)
+
+        xs_dealt = reuse.tile([P, PICKED], U8, name="xs_dealt", offset=0, align_bytes=64)
+        nc.vector.tensor_copy(
+            xs_dealt[:].rearrange("p (d v) -> p v d", d=2), xs[:].rearrange("p (v d) -> p v d", d=2)
+        )
+        xw_dealt = sb.tile([P, PICKED], U32, name="xw_dealt", align_bytes=64)
+        for h in range(2):
+            nc.vector.tensor_copy(
+                xw_dealt[:].bitcast(I32).rearrange("p (d v) -> p v d", d=2)[:, h * P : (h + 1) * P, :],
+                xw[h][:].bitcast(I32).rearrange("p (v d) -> p v d", d=2),
+            )
+
+        yg = []
+        for t in range(PACK):
+            w = sb.tile([P, PICKED], F32, name="yg%d" % t)
+            nc.scalar.activation(w[:], yg_ps[t][:], ACT.Copy, scale=0.6)
+            yg.append(w)
+
+        w1_grouped = reuse.tile([P, PACK, P, PACK], BF16, name="w1_grouped", offset=2 * PICKED, align_bytes=64)
+        round_weight(w1_raw, w1_grouped, nc.vector.tensor_copy, 0, P)
+        es = reuse.tile([P, PICKED], U8, name="es", offset=PICKED, align_bytes=64)
+        nc.vector.tensor_copy(es[:], es_table[:].indirect(off_t[:]))
+        w1q = quantize(w1_grouped[:].rearrange("p t m j -> p (t m j)"), 512, "w1q", "buf_c")
+
+        price_table = sb.tile([P, TABLE], F32, name="price_table", tag="buf_b")
+        nc.sync.dma_start(price_table[:], price)
+
+        y_ps = [psum.tile([P, 2, HALF], F32, name="y_ps%d" % u, tag="bank%d" % (4 + u)) for u in range(2)]
+        for t in range(PACK):
+            for d in range(2):
+                mm(y_ps[t // 2][:, t % 2, :], w1q, slice(t * P, (t + 1) * P), (xw_dealt, xs_dealt), half(d), d == 0, d == 1)
+
+        ew = sb.tile([P, PICKED], U32, name="ew", align_bytes=64)
+        nc.vector.tensor_copy(ew[:], ew_table[:].indirect(off_t[:]))
+
+        gs = []
+        for t in range(PACK):
+            if t == PACK - 1:
+                g = reuse.tile([P, PICKED], F32, name="gs%d" % t, offset=2 * PICKED, align_bytes=64)
+            else:
+                g = sb.tile([P, PICKED], F32, name="gs%d" % t)
+            for h in range(2):
+                looked_up = yg[t][:].indirect(half_list(sub_t, h))
+                if t == PACK - 1:
+                    nc.vector.tensor_copy(g[:, half(h)], looked_up)
+                else:
+                    nc.scalar.activation(g[:, half(h)], looked_up, ACT.Copy)
+            gs.append(g)
+
+        hid = sb.tile([P, PACK, HALF], BF16, name="hid")
+        for t in range(PACK):
+            pairs = gs[t][:].rearrange("p (v d) -> p v d", d=2)
+            gsum = reuse.tile([P, HALF], F32, name="gsum%d" % t, offset=3 * TABLE + 4 * HALF * t, align_bytes=64)
+            nc.vector.tensor_tensor(gsum[:], pairs[:, :, 0], pairs[:, :, 1], ALU.add)
+            bask = sb.tile([P, HALF], F32, name="bask%d" % t)
+            nc.vector.tensor_tensor(bask[:], gsum[:], y_ps[t // 2][:, t % 2, :], ALU.add)
+            signed_tanh = sb.tile([P, HALF], F32, name="signed_tanh%d" % t)
+            nc.scalar.activation(signed_tanh[:], bask[:], ACT.Tanh, scale=unit_sign[:, t : t + 1])
+            magnitude = sb.tile([P, HALF], F32, name="magnitude%d" % t)
+            nc.scalar.activation(magnitude[:], bask[:], ACT.Abs, scale=unit_abs[:, t : t + 1])
+            nc.vector.scalar_tensor_tensor(
+                hid[:, t, :], magnitude[:], unit_off[:, t : t + 1], signed_tanh[:], ALU.add, ALU.mult
+            )
+
+        half_price = sb.tile([P, PICKED], F32, name="half_price", tag="bask3")
+        nc.scalar.activation(half_price[:], price_table[:].indirect(off_t[:]), ACT.Copy, scale=0.5)
+
+        hid_grouped = []
+        for h in range(2):
+            grouped = sb.tile([P, P, PACK], BF16, name="hid_grouped%d" % h, align_bytes=64)
+            nc.vector.tensor_copy(
+                grouped[:].rearrange("p (c i) t -> p c t i", i=4),
+                hid[:, :, h * P : (h + 1) * P].rearrange("p t (c i) -> p c t i", i=4),
+            )
+            hid_grouped.append(grouped)
+        hidq = [quantize(hid_grouped[h][:].rearrange("p v t -> p (v t)"), P, "hidq%d" % h) for h in range(2)]
+
+        sc_ps = {}
+        for h in range(2):
+            for e in range(2):
+                acc = psum.tile([P, HALF], F32, name="sc_ps%d%d" % (h, e), tag="bank%d" % ((6 + 2 * h + e) % 8))
+                mm(acc[:], hidq[h], slice(0, P), (ew, es), half(e), True, True)
+                sc_ps[h, e] = acc
+
+        quarter, own = [], []
+        for h in range(2):
+            quarter.append(sb.tile([P, PICKED], F32, name="quarter%d" % h))
+            own.append(sb.tile([P, PICKED], F32, name="own%d" % h))
+            for e in range(2):
+                o = 1 - e
+                nc.scalar.activation(quarter[h][:, half(e)], sc_ps[h, e][:], ACT.Copy, scale=0.25)
+                nc.vector.scalar_tensor_tensor(
+                    own[h][:, half(o)], sc_ps[h, o][:], 0.5, half_price[:, half(o)], ALU.mult, ALU.subtract
+                )
+
+        arg, fetched = {}, {}
+        for h in range(2):
+            arg[h, 0] = sb.tile([P, HALF], F32, name="arg%d0" % h)
+            nc.vector.tensor_tensor(arg[h, 0][:], quarter[h][:].indirect(half_list(cmp_t, 0)), own[h][:, half(0)], ALU.add)
+            fetched[h] = sb.tile([P, HALF], F32, name="fetched%d" % h)
+            nc.scalar.activation(fetched[h][:], quarter[h][:].indirect(half_list(cmp_t, 1)), ACT.Copy)
+        for h in range(2):
+            arg[h, 1] = sb.tile([P, HALF], F32, name="arg%d1" % h)
+            nc.vector.tensor_tensor(arg[h, 1][:], fetched[h][:], own[h][:, half(1)], ALU.add)
+        for e in range(2):
+            for h in range(2):
+                th = sb.tile([P, HALF], F32, name="tanh%d%d" % (h, e))
+                nc.scalar.activation(th[:], arg[h, e][:], ACT.Tanh)
+                res = sb.tile([P, HALF], F32, name="res%d%d" % (h, e))
+                nc.vector.scalar_tensor_tensor(res[:], th[:], 1.0, half_price[:, half(e)], ALU.add, ALU.mult)
+                nc.sync.dma_start(out[h * P : (h + 1) * P, half(e)], res[:])

@@ -83,7 +83,7 @@ def tile_picked_ybundle_rev_p_kernel(
         nc.sync.dma_start(unit_t[:], unit.rearrange("(p t) o -> p (t o)", t=PACK))
         offs_t = load_list(offs, "offs_t")
         off_t = load_list(off, "off_t")
-        w2_raw = sb.tile([P, PACK, 512], F32, name="w2_raw", tag="buf_c", align_bytes=64)
+        w2_raw = sb.tile([P, PACK, 512], F32, name="w2_raw")
         load_weight(w2_raw, w2)
         sub_t = load_list(sub_, "sub_t")
         cmp_t = load_list(cmp, "cmp_t")
@@ -94,23 +94,25 @@ def tile_picked_ybundle_rev_p_kernel(
         nc.vector.tensor_scalar(positive[:], unit_t[:], 0.0, 2.0, ALU.is_ge, ALU.mult)
         unit_abs = sb.tile([P, PACK], F32, name="unit_abs")
         nc.scalar.activation(unit_abs[:], unit_t[:], ACT.Abs)
-        unit_off = sb.tile([P, PACK], F32, name="unit_off")
-        nc.scalar.activation(unit_off[:], unit_t[:], ACT.Abs, scale=0.4)
+        scaled = sb.tile([P, PACK], F32, name="scaled", tag="buf_e", align_bytes=64)
+        nc.vector.tensor_scalar(scaled[:], unit_t[:], 0.4, None, ALU.mult)
         unit_sign = sb.tile([P, PACK], F32, name="unit_sign")
         nc.scalar.activation(unit_sign[:], positive[:], ACT.Copy, bias=-1.0)
+        unit_off = sb.tile([P, PACK], F32, name="unit_off")
+        nc.vector.tensor_tensor(unit_off[:], scaled[:], unit_sign[:], ALU.mult)
 
         xw_table = reuse.tile([P, TABLE], U32, name="xw_table", offset=0, align_bytes=64)
         load_word_table(xw_table, x_words)
         w1_raw = sb.tile([P, PACK, 512], F32, name="w1_raw", tag="buf_b")
         load_weight(w1_raw, w1)
+        es_table = sb.tile([P, TABLE], U8, name="es_table", tag="buf_e", align_bytes=64)
+        load_scale_table(es_table, e_scales, nc.vector)
 
         w2_grouped = sb.tile([P, PACK, P, PACK], BF16, name="w2_grouped", align_bytes=64)
         round_weight(w2_raw, w2_grouped, nc.vector.tensor_copy, 0, 40)
         round_weight(w2_raw, w2_grouped, nc.scalar.copy, 40, P)
         xs = sb.tile([P, PICKED], U8, name="xs", align_bytes=64)
         nc.vector.tensor_copy(xs[:], xs_table[:].indirect(offs_t[:]))
-        es_table = sb.tile([P, TABLE], U8, name="es_table", tag="buf_c", align_bytes=64)
-        load_scale_table(es_table, e_scales, nc.gpsimd)
         w2q = quantize(w2_grouped[:].rearrange("p t m j -> p (t m j)"), 512, "w2q", "buf_d")
 
         xw = []
@@ -123,10 +125,9 @@ def tile_picked_ybundle_rev_p_kernel(
         load_word_table(ew_table, e_words)
 
         yg_ps = [psum.tile([P, PICKED], F32, name="yg_ps%d" % t, tag="bank%d" % t) for t in range(PACK)]
-        for pair in range(2):
+        for t in range(PACK):
             for h in range(2):
-                for t in (2 * pair, 2 * pair + 1):
-                    mm(yg_ps[t][:, half(h)], w2q, slice(t * P, (t + 1) * P), (xw[h], xs[:, half(h)]), slice(0, HALF), True, True)
+                mm(yg_ps[t][:, half(h)], w2q, slice(t * P, (t + 1) * P), (xw[h], xs[:, half(h)]), slice(0, HALF), True, True)
 
         xs_dealt = reuse.tile([P, PICKED], U8, name="xs_dealt", offset=0, align_bytes=64)
         nc.vector.tensor_copy(
@@ -149,7 +150,7 @@ def tile_picked_ybundle_rev_p_kernel(
         round_weight(w1_raw, w1_grouped, nc.vector.tensor_copy, 0, P)
         es = reuse.tile([P, PICKED], U8, name="es", offset=PICKED, align_bytes=64)
         nc.vector.tensor_copy(es[:], es_table[:].indirect(off_t[:]))
-        w1q = quantize(w1_grouped[:].rearrange("p t m j -> p (t m j)"), 512, "w1q", "buf_c")
+        w1q = quantize(w1_grouped[:].rearrange("p t m j -> p (t m j)"), 512, "w1q", "buf_e")
 
         price_table = sb.tile([P, TABLE], F32, name="price_table", tag="buf_b")
         nc.sync.dma_start(price_table[:], price)
@@ -170,7 +171,7 @@ def tile_picked_ybundle_rev_p_kernel(
                 g = sb.tile([P, PICKED], F32, name="gs%d" % t)
             for h in range(2):
                 looked_up = yg[t][:].indirect(half_list(sub_t, h))
-                if t == PACK - 1:
+                if t == PACK - 1 and h == 1:
                     nc.vector.tensor_copy(g[:, half(h)], looked_up)
                 else:
                     nc.scalar.activation(g[:, half(h)], looked_up, ACT.Copy)
@@ -184,12 +185,15 @@ def tile_picked_ybundle_rev_p_kernel(
             bask = sb.tile([P, HALF], F32, name="bask%d" % t)
             nc.vector.tensor_tensor(bask[:], gsum[:], y_ps[t // 2][:, t % 2, :], ALU.add)
             signed_tanh = sb.tile([P, HALF], F32, name="signed_tanh%d" % t)
-            nc.scalar.activation(signed_tanh[:], bask[:], ACT.Tanh, scale=unit_sign[:, t : t + 1])
             magnitude = sb.tile([P, HALF], F32, name="magnitude%d" % t)
-            nc.scalar.activation(magnitude[:], bask[:], ACT.Abs, scale=unit_abs[:, t : t + 1])
-            nc.vector.scalar_tensor_tensor(
-                hid[:, t, :], magnitude[:], unit_off[:, t : t + 1], signed_tanh[:], ALU.add, ALU.mult
-            )
+            width = P if t == PACK - 1 else HALF
+            for v0 in range(0, HALF, width):
+                v = slice(v0, v0 + width)
+                nc.scalar.activation(signed_tanh[:, v], bask[:, v], ACT.Tanh, scale=unit_sign[:, t : t + 1])
+                nc.scalar.activation(magnitude[:, v], bask[:, v], ACT.Abs, scale=unit_abs[:, t : t + 1])
+                nc.vector.scalar_tensor_tensor(
+                    hid[:, t, v], magnitude[:, v], unit_off[:, t : t + 1], signed_tanh[:, v], ALU.add, ALU.mult
+                )
 
         half_price = sb.tile([P, PICKED], F32, name="half_price", tag="bask3")
         nc.scalar.activation(half_price[:], price_table[:].indirect(off_t[:]), ACT.Copy, scale=0.5)

@@ -109,8 +109,8 @@ def tile_picked_ybundle_rev_p_kernel(
         load_scale_table(es_table, e_scales, nc.vector)
 
         w2_grouped = sb.tile([P, PACK, P, PACK], BF16, name="w2_grouped", align_bytes=64)
-        round_weight(w2_raw, w2_grouped, nc.vector.tensor_copy, 0, 40)
-        round_weight(w2_raw, w2_grouped, nc.scalar.copy, 40, P)
+        round_weight(w2_raw, w2_grouped, nc.vector.tensor_copy, 0, 48)
+        round_weight(w2_raw, w2_grouped, nc.scalar.copy, 48, P)
         xs = sb.tile([P, PICKED], U8, name="xs", align_bytes=64)
         nc.vector.tensor_copy(xs[:], xs_table[:].indirect(offs_t[:]))
         w2q = quantize(w2_grouped[:].rearrange("p t m j -> p (t m j)"), 512, "w2q", "buf_d")
@@ -171,32 +171,44 @@ def tile_picked_ybundle_rev_p_kernel(
                 g = sb.tile([P, PICKED], F32, name="gs%d" % t)
             for h in range(2):
                 looked_up = yg[t][:].indirect(half_list(sub_t, h))
-                if t == PACK - 1 and h == 1:
+                if t == PACK - 1:
                     nc.vector.tensor_copy(g[:, half(h)], looked_up)
                 else:
                     nc.scalar.activation(g[:, half(h)], looked_up, ACT.Copy)
             gs.append(g)
 
         hid = sb.tile([P, PACK, HALF], BF16, name="hid")
+        basks = []
         for t in range(PACK):
             pairs = gs[t][:].rearrange("p (v d) -> p v d", d=2)
-            gsum = reuse.tile([P, HALF], F32, name="gsum%d" % t, offset=3 * TABLE + 4 * HALF * t, align_bytes=64)
-            nc.vector.tensor_tensor(gsum[:], pairs[:, :, 0], pairs[:, :, 1], ALU.add)
-            bask = sb.tile([P, HALF], F32, name="bask%d" % t)
+            if t < 3:
+                gsum = sb.tile([P, HALF], F32, name="gsum%d" % t)
+            else:
+                gsum = reuse.tile([P, HALF], F32, name="gsum%d" % t, offset=3 * TABLE + 4 * HALF * t, align_bytes=64)
+            adder = nc.gpsimd if t < 3 else nc.vector
+            adder.tensor_tensor(gsum[:], pairs[:, :, 0], pairs[:, :, 1], ALU.add)
+            if t < 2:
+                bask = reuse.tile([P, HALF], F32, name="bask%d" % t, offset=3 * TABLE + 4 * HALF * t, align_bytes=64)
+            else:
+                bask = sb.tile([P, HALF], F32, name="bask%d" % t)
             nc.vector.tensor_tensor(bask[:], gsum[:], y_ps[t // 2][:, t % 2, :], ALU.add)
-            signed_tanh = sb.tile([P, HALF], F32, name="signed_tanh%d" % t)
-            magnitude = sb.tile([P, HALF], F32, name="magnitude%d" % t)
-            width = P if t == PACK - 1 else HALF
-            for v0 in range(0, HALF, width):
-                v = slice(v0, v0 + width)
-                nc.scalar.activation(signed_tanh[:, v], bask[:, v], ACT.Tanh, scale=unit_sign[:, t : t + 1])
-                nc.scalar.activation(magnitude[:, v], bask[:, v], ACT.Abs, scale=unit_abs[:, t : t + 1])
-                nc.vector.scalar_tensor_tensor(
-                    hid[:, t, v], magnitude[:, v], unit_off[:, t : t + 1], signed_tanh[:, v], ALU.add, ALU.mult
-                )
+            basks.append(bask)
 
-        half_price = sb.tile([P, PICKED], F32, name="half_price", tag="bask3")
-        nc.scalar.activation(half_price[:], price_table[:].indirect(off_t[:]), ACT.Copy, scale=0.5)
+        pieces = [(t, slice(0, HALF)) for t in range(2)]
+        pieces += [(t, slice(h * P, (h + 1) * P)) for h in range(2) for t in range(2, PACK)]
+        signed_tanh = sb.tile([P, PACK, HALF], F32, name="signed_tanh")
+        magnitude = sb.tile([P, PACK, HALF], F32, name="magnitude")
+        for t, v in pieces:
+            nc.scalar.activation(signed_tanh[:, t, v], basks[t][:, v], ACT.Tanh, scale=unit_sign[:, t : t + 1])
+            nc.scalar.activation(magnitude[:, t, v], basks[t][:, v], ACT.Abs, scale=unit_abs[:, t : t + 1])
+            nc.vector.scalar_tensor_tensor(
+                hid[:, t, v], magnitude[:, t, v], unit_off[:, t : t + 1], signed_tanh[:, t, v], ALU.add, ALU.mult
+            )
+
+        half_price = {}
+        for e in (1, 0):
+            half_price[e] = sb.tile([P, HALF], F32, name="half_price%d" % e, tag="bask%d" % (3 - e))
+            nc.scalar.activation(half_price[e][:], price_table[:].indirect(half_list(off_t, e)), ACT.Copy, scale=0.5)
 
         hid_grouped = []
         for h in range(2):
@@ -218,12 +230,12 @@ def tile_picked_ybundle_rev_p_kernel(
         quarter, own = [], []
         for h in range(2):
             quarter.append(sb.tile([P, PICKED], F32, name="quarter%d" % h))
-            own.append(sb.tile([P, PICKED], F32, name="own%d" % h))
+            own.append(sb.tile([P, PICKED], F32, name="own%d" % h, tag="hid_grouped%d" % (1 - h), align_bytes=64))
             for e in range(2):
                 o = 1 - e
                 nc.scalar.activation(quarter[h][:, half(e)], sc_ps[h, e][:], ACT.Copy, scale=0.25)
                 nc.vector.scalar_tensor_tensor(
-                    own[h][:, half(o)], sc_ps[h, o][:], 0.5, half_price[:, half(o)], ALU.mult, ALU.subtract
+                    own[h][:, half(o)], sc_ps[h, o][:], 0.5, half_price[o][:], ALU.mult, ALU.subtract
                 )
 
         arg, fetched = {}, {}
@@ -240,5 +252,5 @@ def tile_picked_ybundle_rev_p_kernel(
                 th = sb.tile([P, HALF], F32, name="tanh%d%d" % (h, e))
                 nc.scalar.activation(th[:], arg[h, e][:], ACT.Tanh)
                 res = sb.tile([P, HALF], F32, name="res%d%d" % (h, e))
-                nc.vector.scalar_tensor_tensor(res[:], th[:], 1.0, half_price[:, half(e)], ALU.add, ALU.mult)
+                nc.vector.scalar_tensor_tensor(res[:], th[:], 1.0, half_price[e][:], ALU.add, ALU.mult)
                 nc.sync.dma_start(out[h * P : (h + 1) * P, half(e)], res[:])

@@ -109,8 +109,8 @@ def tile_picked_ybundle_rev_p_kernel(
         load_scale_table(es_table, e_scales, nc.vector)
 
         w2_grouped = sb.tile([P, PACK, P, PACK], BF16, name="w2_grouped", align_bytes=64)
-        round_weight(w2_raw, w2_grouped, nc.vector.tensor_copy, 0, 48)
-        round_weight(w2_raw, w2_grouped, nc.scalar.copy, 48, P)
+        round_weight(w2_raw, w2_grouped, nc.vector.tensor_copy, 0, 40)
+        round_weight(w2_raw, w2_grouped, nc.scalar.copy, 40, P)
         xs = sb.tile([P, PICKED], U8, name="xs", align_bytes=64)
         nc.vector.tensor_copy(xs[:], xs_table[:].indirect(offs_t[:]))
         w2q = quantize(w2_grouped[:].rearrange("p t m j -> p (t m j)"), 512, "w2q", "buf_d")
@@ -171,7 +171,7 @@ def tile_picked_ybundle_rev_p_kernel(
                 g = sb.tile([P, PICKED], F32, name="gs%d" % t)
             for h in range(2):
                 looked_up = yg[t][:].indirect(half_list(sub_t, h))
-                if t == PACK - 1:
+                if t == PACK - 1 and h == 1:
                     nc.vector.tensor_copy(g[:, half(h)], looked_up)
                 else:
                     nc.scalar.activation(g[:, half(h)], looked_up, ACT.Copy)
@@ -181,16 +181,10 @@ def tile_picked_ybundle_rev_p_kernel(
         basks = []
         for t in range(PACK):
             pairs = gs[t][:].rearrange("p (v d) -> p v d", d=2)
-            if t < 3:
-                gsum = sb.tile([P, HALF], F32, name="gsum%d" % t)
-            else:
-                gsum = reuse.tile([P, HALF], F32, name="gsum%d" % t, offset=3 * TABLE + 4 * HALF * t, align_bytes=64)
-            adder = nc.gpsimd if t < 3 else nc.vector
+            gsum = sb.tile([P, HALF], F32, name="gsum%d" % t, tag="gsum%d" % (1 if t == PACK - 1 else t))
+            adder = nc.gpsimd if t < PACK - 1 else nc.vector
             adder.tensor_tensor(gsum[:], pairs[:, :, 0], pairs[:, :, 1], ALU.add)
-            if t < 2:
-                bask = reuse.tile([P, HALF], F32, name="bask%d" % t, offset=3 * TABLE + 4 * HALF * t, align_bytes=64)
-            else:
-                bask = sb.tile([P, HALF], F32, name="bask%d" % t)
+            bask = reuse.tile([P, HALF], F32, name="bask%d" % t, offset=3 * TABLE + 4 * HALF * t, align_bytes=64)
             nc.vector.tensor_tensor(bask[:], gsum[:], y_ps[t // 2][:, t % 2, :], ALU.add)
             basks.append(bask)
 
@@ -207,7 +201,7 @@ def tile_picked_ybundle_rev_p_kernel(
 
         half_price = {}
         for e in (1, 0):
-            half_price[e] = sb.tile([P, HALF], F32, name="half_price%d" % e, tag="bask%d" % (3 - e))
+            half_price[e] = reuse.tile([P, HALF], F32, name="half_price%d" % e, offset=3 * TABLE + 4 * HALF * (3 - e), align_bytes=64)
             nc.scalar.activation(half_price[e][:], price_table[:].indirect(half_list(off_t, e)), ACT.Copy, scale=0.5)
 
         hid_grouped = []

@@ -165,13 +165,13 @@ def tile_picked_ybundle_rev_p_kernel(
 
         gs = []
         for t in range(PACK):
-            if t == PACK - 1:
+            if t == 1:
                 g = reuse.tile([P, PICKED], F32, name="gs%d" % t, offset=2 * PICKED, align_bytes=64)
             else:
                 g = sb.tile([P, PICKED], F32, name="gs%d" % t)
             for h in range(2):
                 looked_up = yg[t][:].indirect(half_list(sub_t, h))
-                if t == PACK - 1 and h == 1:
+                if t == 1:
                     nc.vector.tensor_copy(g[:, half(h)], looked_up)
                 else:
                     nc.scalar.activation(g[:, half(h)], looked_up, ACT.Copy)

from contextlib import ExitStack

import concourse.mybir as mybir

F32 = mybir.dt.float32
BF16 = mybir.dt.bfloat16
I32 = mybir.dt.int32
U32 = mybir.dt.uint32
U16 = mybir.dt.uint16
U8 = mybir.dt.uint8
FP8X4 = mybir.dt.float8_e4m3fn_x4
ALU = mybir.AluOpType
ACT = mybir.ActivationFunctionType

P = 128
PACK = 4
K = 512
TABLE = 2048
PICKED = 512
HALF = 256
LIST_COLS = PICKED // 16
FLOPS = 2 * K * 512 * PICKED * 2 + 2 * 512 * 256 * PICKED


def tile_picked_ybundle_rev_p_kernel(
    tc, x_words, x_scales, w1, w2, e_words, e_scales, unit, price, offs, sub_, off, cmp, out
):
    nc = tc.nc
    with ExitStack() as ctx:
        lists = ctx.enter_context(tc.tile_pool(name="lists", bufs=1))
        sb = ctx.enter_context(tc.tile_pool(name="sb", bufs=1))
        reuse = ctx.enter_context(tc.tile_pool(name="reuse", bufs=1))
        psum = ctx.enter_context(tc.psum_pool(name="psum", bufs=1))

        def load_list(src, name):
            t = lists.tile([P, LIST_COLS], U16, name=name)
            nc.sync.dma_start(t[:], src)
            return t

        def half_list(lst, h):
            return lst[:, h * (LIST_COLS // 2) : (h + 1) * (LIST_COLS // 2)]

        def half(h):
            return slice(h * HALF, (h + 1) * HALF)

        def load_scale_table(t, src, clear_engine):
            as_words = t[:].bitcast(I32)
            clear_engine.memset(as_words, 0)
            rows = src[0].bitcast(I32)
            for q in range(4):
                nc.sync.dma_start(as_words[32 * q : 32 * q + 4, :], rows[4 * q : 4 * q + 4, :])

        def load_word_table(t, src):
            nc.sync.dma_start(t[:].bitcast(I32), src[0].rearrange("p n t -> p (n t)").bitcast(I32))

        def load_weight(t, src):
            nc.sync.dma_start(t[:], src.rearrange("(p j) c -> p j c", j=PACK))

        def round_weight(raw, grouped, engine_copy, m0, m1):
            engine_copy(
                grouped[:].rearrange("p t m j -> p m j t")[:, m0:m1],
                raw[:].rearrange("p j (m t) -> p m j t", t=PACK)[:, m0:m1],
            )

        def quantize(grouped_ap, width, name, tag=""):
            codes = sb.tile([P, width], U32, name=name + "_codes", tag=tag, align_bytes=64)
            scales = sb.tile([P, width], U8, name=name + "_scales", align_bytes=64)
            nc.vector.quantize_mx(out=codes[:].bitcast(FP8X4), scales=scales[:], in_=grouped_ap)
            return codes, scales

        def mm(acc, lhs, lcols, rhs, rcols, start, stop):
            nc.tensor.matmul_mx(
                out=acc,
                lhsT=lhs[0][:, lcols].bitcast(FP8X4),
                lhsT_scale=lhs[1][:, lcols],
                rhs=rhs[0][:, rcols].bitcast(FP8X4),
                rhs_scale=rhs[1][:, rcols],
                start=start,
                stop=stop,
            )

        unit_t = reuse.tile([P, PACK], F32, name="unit_t", offset=0, align_bytes=64)
        nc.sync.dma_start(unit_t[:], unit.rearrange("(p t) o -> p (t o)", t=PACK))
        offs_t = load_list(offs, "offs_t")
        off_t = load_list(off, "off_t")
        w2_raw = sb.tile([P, PACK, 512], F32, name="w2_raw")
        load_weight(w2_raw, w2)
        sub_t = load_list(sub_, "sub_t")
        cmp_t = load_list(cmp, "cmp_t")
        xs_table = sb.tile([P, TABLE], U8, name="xs_table", tag="buf_d", align_bytes=64)
        load_scale_table(xs_table, x_scales, nc.vector)

        positive = sb.tile([P, PACK], F32, name="positive", tag="buf_b")
        nc.vector.tensor_scalar(positive[:], unit_t[:], 0.0, 2.0, ALU.is_ge, ALU.mult)
        unit_abs = sb.tile([P, PACK], F32, name="unit_abs")
        nc.scalar.activation(unit_abs[:], unit_t[:], ACT.Abs)
        scaled = sb.tile([P, PACK], F32, name="scaled", tag="buf_e", align_bytes=64)
        nc.vector.tensor_scalar(scaled[:], unit_t[:], 0.4, None, ALU.mult)
        unit_sign = sb.tile([P, PACK], F32, name="unit_sign")
        nc.scalar.activation(unit_sign[:], positive[:], ACT.Copy, bias=-1.0)
        unit_off = sb.tile([P, PACK], F32, name="unit_off")
        nc.vector.tensor_tensor(unit_off[:], scaled[:], unit_sign[:], ALU.mult)

        xw_table = reuse.tile([P, TABLE], U32, name="xw_table", offset=0, align_bytes=64)
        load_word_table(xw_table, x_words)
        w1_raw = sb.tile([P, PACK, 512], F32, name="w1_raw", tag="buf_b")
        load_weight(w1_raw, w1)
        es_table = sb.tile([P, TABLE], U8, name="es_table", tag="buf_e", align_bytes=64)
        load_scale_table(es_table, e_scales, nc.vector)

        w2_grouped = sb.tile([P, PACK, P, PACK], BF16, name="w2_grouped", align_bytes=64)
        round_weight(w2_raw, w2_grouped, nc.vector.tensor_copy, 0, 40)
        round_weight(w2_raw, w2_grouped, nc.scalar.copy, 40, P)
        xs = sb.tile([P, PICKED], U8, name="xs", align_bytes=64)
        nc.vector.tensor_copy(xs[:], xs_table[:].indirect(offs_t[:]))
        w2q = quantize(w2_grouped[:].rearrange("p t m j -> p (t m j)"), 512, "w2q", "buf_d")

        xw = []
        for h in range(2):
            picked = sb.tile([P, HALF], U32, name="xw%d" % h, align_bytes=64)
            nc.vector.tensor_copy(picked[:], xw_table[:].indirect(half_list(offs_t, h)))
            xw.append(picked)

        ew_table = reuse.tile([P, TABLE], U32, name="ew_table", offset=3 * TABLE, align_bytes=64)
        load_word_table(ew_table, e_words)

        yg_ps = [psum.tile([P, PICKED], F32, name="yg_ps%d" % t, tag="bank%d" % t) for t in range(PACK)]
        for t in range(PACK):
            for h in range(2):
                mm(yg_ps[t][:, half(h)], w2q, slice(t * P, (t + 1) * P), (xw[h], xs[:, half(h)]), slice(0, HALF), True, True)

        xs_dealt = reuse.tile([P, PICKED], U8, name="xs_dealt", offset=0, align_bytes=64)
        nc.vector.tensor_copy(
            xs_dealt[:].rearrange("p (d v) -> p v d", d=2), xs[:].rearrange("p (v d) -> p v d", d=2)
        )
        xw_dealt = sb.tile([P, PICKED], U32, name="xw_dealt", align_bytes=64)
        for h in range(2):
            nc.vector.tensor_copy(
                xw_dealt[:].bitcast(I32).rearrange("p (d v) -> p v d", d=2)[:, h * P : (h + 1) * P, :],
                xw[h][:].bitcast(I32).rearrange("p (v d) -> p v d", d=2),
            )

        yg = []
        for t in range(PACK):
            w = sb.tile([P, PICKED], F32, name="yg%d" % t)
            nc.scalar.activation(w[:], yg_ps[t][:], ACT.Copy, scale=0.6)
            yg.append(w)

        w1_grouped = reuse.tile([P, PACK, P, PACK], BF16, name="w1_grouped", offset=2 * PICKED, align_bytes=64)
        round_weight(w1_raw, w1_grouped, nc.vector.tensor_copy, 0, P)
        es = reuse.tile([P, PICKED], U8, name="es", offset=PICKED, align_bytes=64)
        nc.vector.tensor_copy(es[:], es_table[:].indirect(off_t[:]))
        w1q = quantize(w1_grouped[:].rearrange("p t m j -> p (t m j)"), 512, "w1q", "buf_e")

        price_table = sb.tile([P, TABLE], F32, name="price_table", tag="buf_b")
        nc.sync.dma_start(price_table[:], price)

        y_ps = [psum.tile([P, 2, HALF], F32, name="y_ps%d" % u, tag="bank%d" % (4 + u)) for u in range(2)]
        for t in range(PACK):
            for d in range(2):
                mm(y_ps[t // 2][:, t % 2, :], w1q, slice(t * P, (t + 1) * P), (xw_dealt, xs_dealt), half(d), d == 0, d == 1)

        ew = sb.tile([P, PICKED], U32, name="ew", align_bytes=64)
        nc.vector.tensor_copy(ew[:], ew_table[:].indirect(off_t[:]))

        gs = []
        for t in range(PACK):
            if t == 1:
                g = reuse.tile([P, PICKED], F32, name="gs%d" % t, offset=2 * PICKED, align_bytes=64)
            else:
                g = sb.tile([P, PICKED], F32, name="gs%d" % t)
            for h in range(2):
                looked_up = yg[t][:].indirect(half_list(sub_t, h))
                if t == 1:
                    nc.vector.tensor_copy(g[:, half(h)], looked_up)
                else:
                    nc.scalar.activation(g[:, half(h)], looked_up, ACT.Copy)
            gs.append(g)

        hid = sb.tile([P, PACK, HALF], BF16, name="hid")
        basks = []
        for t in range(PACK):
            pairs = gs[t][:].rearrange("p (v d) -> p v d", d=2)
            gsum = sb.tile([P, HALF], F32, name="gsum%d" % t, tag="gsum%d" % (1 if t == PACK - 1 else t))
            adder = nc.gpsimd if t < PACK - 1 else nc.vector
            adder.tensor_tensor(gsum[:], pairs[:, :, 0], pairs[:, :, 1], ALU.add)
            bask = reuse.tile([P, HALF], F32, name="bask%d" % t, offset=3 * TABLE + 4 * HALF * t, align_bytes=64)
            nc.vector.tensor_tensor(bask[:], gsum[:], y_ps[t // 2][:, t % 2, :], ALU.add)
            basks.append(bask)

        pieces = [(t, slice(0, HALF)) for t in range(2)]
        pieces += [(t, slice(h * P, (h + 1) * P)) for h in range(2) for t in range(2, PACK)]
        signed_tanh = sb.tile([P, PACK, HALF], F32, name="signed_tanh")
        magnitude = sb.tile([P, PACK, HALF], F32, name="magnitude")
        for t, v in pieces:
            nc.scalar.activation(signed_tanh[:, t, v], basks[t][:, v], ACT.Tanh, scale=unit_sign[:, t : t + 1])
            nc.scalar.activation(magnitude[:, t, v], basks[t][:, v], ACT.Abs, scale=unit_abs[:, t : t + 1])
            nc.vector.scalar_tensor_tensor(
                hid[:, t, v], magnitude[:, t, v], unit_off[:, t : t + 1], signed_tanh[:, t, v], ALU.add, ALU.mult
            )

        half_price = {}
        for e in (1, 0):
            half_price[e] = reuse.tile([P, HALF], F32, name="half_price%d" % e, offset=3 * TABLE + 4 * HALF * (3 - e), align_bytes=64)
            nc.scalar.activation(half_price[e][:], price_table[:].indirect(half_list(off_t, e)), ACT.Copy, scale=0.5)

        hid_grouped = []
        for h in range(2):
            grouped = sb.tile([P, P, PACK], BF16, name="hid_grouped%d" % h, align_bytes=64)
            nc.vector.tensor_copy(
                grouped[:].rearrange("p (c i) t -> p c t i", i=4),
                hid[:, :, h * P : (h + 1) * P].rearrange("p t (c i) -> p c t i", i=4),
            )
            hid_grouped.append(grouped)
        hidq = [quantize(hid_grouped[h][:].rearrange("p v t -> p (v t)"), P, "hidq%d" % h) for h in range(2)]

        sc_ps = {}
        for h in range(2):
            for e in range(2):
                acc = psum.tile([P, HALF], F32, name="sc_ps%d%d" % (h, e), tag="bank%d" % ((6 + 2 * h + e) % 8))
                mm(acc[:], hidq[h], slice(0, P), (ew, es), half(e), True, True)
                sc_ps[h, e] = acc

        quarter, own = [], []
        for h in range(2):
            quarter.append(sb.tile([P, PICKED], F32, name="quarter%d" % h))
            own.append(sb.tile([P, PICKED], F32, name="own%d" % h, tag="hid_grouped%d" % (1 - h), align_bytes=64))
            for e in range(2):
                o = 1 - e
                nc.scalar.activation(quarter[h][:, half(e)], sc_ps[h, e][:], ACT.Copy, scale=0.25)
                nc.vector.scalar_tensor_tensor(
                    own[h][:, half(o)], sc_ps[h, o][:], 0.5, half_price[o][:], ALU.mult, ALU.subtract
                )

        arg, fetched = {}, {}
        for h in range(2):
            arg[h, 0] = sb.tile([P, HALF], F32, name="arg%d0" % h)
            nc.vector.tensor_tensor(arg[h, 0][:], quarter[h][:].indirect(half_list(cmp_t, 0)), own[h][:, half(0)], ALU.add)
            fetched[h] = sb.tile([P, HALF], F32, name="fetched%d" % h)
            nc.scalar.activation(fetched[h][:], quarter[h][:].indirect(half_list(cmp_t, 1)), ACT.Copy)
        for h in range(2):
            arg[h, 1] = sb.tile([P, HALF], F32, name="arg%d1" % h)
            nc.vector.tensor_tensor(arg[h, 1][:], fetched[h][:], own[h][:, half(1)], ALU.add)
        for e in range(2):
            for h in range(2):
                th = sb.tile([P, HALF], F32, name="tanh%d%d" % (h, e))
                nc.scalar.activation(th[:], arg[h, e][:], ACT.Tanh)
                res = sb.tile([P, HALF], F32, name="res%d%d" % (h, e))
                nc.vector.scalar_tensor_tensor(res[:], th[:], 1.0, half_price[e][:], ALU.add, ALU.mult)
                nc.sync.dma_start(out[h * P : (h + 1) * P, half(e)], res[:])
